import numpy as np, ml_dtypes
CORES = [30,158,46,174,86,214]
N = 6
import mx_ref
NC, KT = 512, 2
FROM = [1,5,3,2,0,4]
BF = ml_dtypes.bfloat16
def setup_inputs(rng):
    def f(*shape):
        return mx_ref.flush((rng.standard_normal(shape, dtype=np.float32) * np.exp2(rng.integers(-2, 3, shape[:-1] + (1,)))).astype(BF))
    return {"w": f(N, 128, KT * 512), "x": f(N, 128, KT * 4 * NC)}
def setup_inputs_blocks(rng):
    d = setup_inputs(rng)
    for k in ("w", "x"): d[k] = mx_ref.spread(d[k], rng, 4)
    return d
def setup_inputs_wide(rng):
    d = setup_inputs(rng)
    for k in ("w", "x"): d[k] = mx_ref.flush((d[k].astype(np.float32) * np.exp2(rng.integers(-8, 9, (N, 1, 1))).astype(np.float32)).astype(BF))
    return d
def setup_inputs_zeros(rng):
    d = setup_inputs(rng); v = d["x"].reshape(N, 128, -1, 4).copy()
    v[np.broadcast_to((rng.random((N, 1, v.shape[2], 1)) < 0.33), v.shape)] = 0
    d["x"] = v.reshape(d["x"].shape)
    return d
def reference(w, x):
    y = np.zeros((N, 128, NC), np.float32)
    for r in range(N):
        for t in range(KT):
            p = mx_ref.matmul(mx_ref.quantize(w[r][:, 512 * t:512 * t + 512]), mx_ref.quantize(x[FROM[r]][:, 4 * NC * t:4 * NC * t + 4 * NC]))
            y[r] = p if t == 0 else y[r] + p
    return {"y": y}

@@ -1,0 +1,86 @@
+from concourse.mybir import dt
+
+NC = 512
+KT = 2
+GROUPS = [(0, 256), (256, 512)]
+G = len(GROUPS)
+
+SCRATCH = {
+    "xb": ("sbuf", [128, KT * 4 * NC], "bfloat16"),
+    "wb": ("sbuf", [128, KT * 512], "bfloat16"),
+    "xq": ("sbuf", [128, KT * NC], "float8_e4m3fn_x4"),
+    "xs": ("sbuf", [128, KT * NC], "uint8"),
+    "wq": ("sbuf", [128, KT * 128], "float8_e4m3fn_x4"),
+    "ws": ("sbuf", [128, KT * 128], "uint8"),
+    "rq": ("sbuf", [128, KT * NC], "float8_e4m3fn_x4"),
+    "rs": ("sbuf", [128, KT * NC], "uint8"),
+    "ps": ("psum", [128, 512 * G], "float32"),
+    "yb": ("sbuf", [128, NC], "float32"),
+}
+SEMAPHORES = (["lx%d_%d" % (k, t) for k in range(G) for t in range(KT)]
+              + ["q%d" % k for k in range(G)] + ["arr%d" % k for k in range(G)]
+              + ["mm%d" % k for k in range(G)] + ["cp%d" % k for k in range(G)]
+              + ["lw", "qw", "st", "sent"])
+
+
+def _engines(mask):
+    return bin(mask).count("1")
+
+
+def rank_program(g, core, T, topo):
+    rank = T.rank_of(core)
+    if rank is None:
+        return
+    frm = T.tables["FROM"]
+    src = T.cores[frm[rank]]
+    dst = T.cores[frm.index(rank)]
+    rid, pid = topo.addr(dst, core)
+    mask = topo.mask(core, dst)
+    n_out, n_in = _engines(mask), _engines(topo.mask(src, core))
+    loaders = (g.sync, g.scalar)
+
+    for k, (c0, c1) in enumerate(GROUPS):
+        for t in range(KT):
+            a, b = 4 * NC * t + 4 * c0, 4 * NC * t + 4 * c1
+            loaders[t % 2].dma_start(T.xb[:, a:b], T.x[:, a:b]).then_inc(T.sem["lx%d_%d" % (k, t)], 16)
+    g.sync.dma_start(T.wb[:, :], T.w[:, :]).then_inc(T.sem.lw, 16)
+
+    for k, (c0, c1) in enumerate(GROUPS):
+        n = c1 - c0
+        for t in range(KT):
+            a, b = 4 * NC * t + 4 * c0, 4 * NC * t + 4 * c1
+            p = KT * c0 + t * n
+            g.vector.wait_ge(T.sem["lx%d_%d" % (k, t)], 16)
+            g.vector.quantize_mx(T.xq[:, p:p + n], T.xs[:, p:p + n], T.xb[:, a:b]).then_inc(T.sem["q%d" % k], 1)
+    g.vector.wait_ge(T.sem.lw, 16)
+    for t in range(KT):
+        g.vector.quantize_mx(T.wq[:, 128 * t:128 * t + 128], T.ws[:, 128 * t:128 * t + 128],
+                             T.wb[:, 512 * t:512 * t + 512]).then_inc(T.sem.qw, 1)
+
+    for k, (c0, c1) in enumerate(GROUPS):
+        a, b = KT * c0, KT * c1
+        g.wait_ge(T.sem["q%d" % k], KT)
+        g.remote_dma(out_ap=T.rs[:, a:b], in_ap=T.xs[:, a:b], remote_sem=T.sem["arr%d" % k], local_sem=T.sem.sent,
+                     pid=pid, routing_id=rid, dma_engine_mask=mask)
+        g.remote_dma(out_ap=T.rq[:, a:b].bitcast(dt.uint8), in_ap=T.xq[:, a:b].bitcast(dt.uint8),
+                     remote_sem=T.sem["arr%d" % k], local_sem=T.sem.sent, pid=pid, routing_id=rid,
+                     dma_engine_mask=mask)
+
+    g.tensor.wait_ge(T.sem.qw, KT)
+    for k, (c0, c1) in enumerate(GROUPS):
+        n = c1 - c0
+        g.tensor.wait_ge(T.sem["arr%d" % k], 2 * n_in)
+        for t in range(KT):
+            p = KT * c0 + t * n
+            g.tensor.matmul_mx(T.ps[:, 512 * k:512 * k + n], T.wq[:, 128 * t:128 * t + 128],
+                               T.ws[:, 128 * t:128 * t + 128], T.rq[:, p:p + n], T.rs[:, p:p + n],
+                               t == 0, t == KT - 1).then_inc(T.sem["mm%d" % k], 1)
+
+    for k, (c0, c1) in enumerate(GROUPS):
+        n = c1 - c0
+        g.vector.wait_ge(T.sem["mm%d" % k], KT)
+        g.vector.tensor_copy(T.yb[:, c0:c1], T.ps[:, 512 * k:512 * k + n]).then_inc(T.sem["cp%d" % k], 1)
+        g.sync.wait_ge(T.sem["cp%d" % k], 1)
+        g.sync.dma_start(T.y[:, c0:c1], T.yb[:, c0:c1]).then_inc(T.sem.st, 16)
+    g.sync.wait_ge(T.sem.st, 16 * G)
+    g.wait_ge(T.sem.sent, 2 * G * n_out)

@@ -2,7 +2,8 @@ from concourse.mybir import dt
 
 NC = 512
 KT = 2
-GROUPS = [(0, 256), (256, 512)]
+GROUPS = [(0, 128), (128, 384), (384, 512)]
+PLANES = [(0, 0), (1, 2)]
 G = len(GROUPS)
 
 SCRATCH = {
@@ -18,7 +19,8 @@ SCRATCH = {
     "yb": ("sbuf", [128, NC], "float32"),
 }
 SEMAPHORES = (["lx%d_%d" % (k, t) for k in range(G) for t in range(KT)]
-              + ["q%d" % k for k in range(G)] + ["arr%d" % k for k in range(G)]
+              + ["q%d" % k for k in range(G)] + ["ac%d" % k for k in range(G)]
+              + ["ap%d" % j for j in range(len(PLANES))]
               + ["mm%d" % k for k in range(G)] + ["cp%d" % k for k in range(G)]
               + ["lw", "qw", "st", "sent"])
 
@@ -58,18 +60,24 @@ def rank_program(g, core, T, topo):
                              T.wb[:, 512 * t:512 * t + 512]).then_inc(T.sem.qw, 1)
 
     for k, (c0, c1) in enumerate(GROUPS):
-        a, b = KT * c0, KT * c1
         g.wait_ge(T.sem["q%d" % k], KT)
-        g.remote_dma(out_ap=T.rs[:, a:b], in_ap=T.xs[:, a:b], remote_sem=T.sem["arr%d" % k], local_sem=T.sem.sent,
-                     pid=pid, routing_id=rid, dma_engine_mask=mask)
+        for j, (k0, k1) in enumerate(PLANES):
+            if k1 == k:
+                a, b = KT * GROUPS[k0][0], KT * GROUPS[k1][1]
+                g.remote_dma(out_ap=T.rs[:, a:b], in_ap=T.xs[:, a:b], remote_sem=T.sem["ap%d" % j],
+                             local_sem=T.sem.sent, pid=pid, routing_id=rid, dma_engine_mask=mask)
+        a, b = KT * c0, KT * c1
         g.remote_dma(out_ap=T.rq[:, a:b].bitcast(dt.uint8), in_ap=T.xq[:, a:b].bitcast(dt.uint8),
-                     remote_sem=T.sem["arr%d" % k], local_sem=T.sem.sent, pid=pid, routing_id=rid,
+                     remote_sem=T.sem["ac%d" % k], local_sem=T.sem.sent, pid=pid, routing_id=rid,
                      dma_engine_mask=mask)
 
     g.tensor.wait_ge(T.sem.qw, KT)
     for k, (c0, c1) in enumerate(GROUPS):
         n = c1 - c0
-        g.tensor.wait_ge(T.sem["arr%d" % k], 2 * n_in)
+        g.tensor.wait_ge(T.sem["ac%d" % k], n_in)
+        for j, (k0, k1) in enumerate(PLANES):
+            if k0 == k:
+                g.tensor.wait_ge(T.sem["ap%d" % j], n_in)
         for t in range(KT):
             p = KT * c0 + t * n
             g.tensor.matmul_mx(T.ps[:, 512 * k:512 * k + n], T.wq[:, 128 * t:128 * t + 128],
@@ -83,4 +91,4 @@ def rank_program(g, core, T, topo):
         g.sync.wait_ge(T.sem["cp%d" % k], 1)
         g.sync.dma_start(T.y[:, c0:c1], T.yb[:, c0:c1]).then_inc(T.sem.st, 16)
     g.sync.wait_ge(T.sem.st, 16 * G)
-    g.wait_ge(T.sem.sent, 2 * G * n_out)
+    g.wait_ge(T.sem.sent, (G + len(PLANES)) * n_out)

@@ -2,8 +2,10 @@ from concourse.mybir import dt
 
 NC = 512
 KT = 2
-GROUPS = [(0, 128), (128, 384), (384, 512)]
-PLANES = [(0, 0), (1, 2)]
+GROUPS = [(0, 128), (128, 256), (256, 384), (384, 512)]
+RELAY = (1,)
+PLANES = [(0, 0), (1, 1), (2, 3)]
+MULT = [0, 2, 1, 3]
 G = len(GROUPS)
 
 SCRATCH = {
@@ -21,6 +23,7 @@ SCRATCH = {
 SEMAPHORES = (["lx%d_%d" % (k, t) for k in range(G) for t in range(KT)]
               + ["q%d" % k for k in range(G)] + ["ac%d" % k for k in range(G)]
               + ["ap%d" % j for j in range(len(PLANES))]
+              + ["hc%d" % k for k in range(G)] + ["hp%d" % j for j in range(len(PLANES))]
               + ["mm%d" % k for k in range(G)] + ["cp%d" % k for k in range(G)]
               + ["lw", "qw", "st", "sent"])
 
@@ -29,16 +32,59 @@ def _engines(mask):
     return bin(mask).count("1")
 
 
+def _helper(T, topo, c, d):
+    hosts = 1 + max(topo.host(k) for k in T.cores)
+    for h in range(hosts * topo.CORES_PER_HOST):
+        if (topo.host(h) == topo.host(c) and topo.chip(h) == topo.chip(c) and h not in T.cores
+                and topo.die(h) != topo.die(c) and topo.may_write(c, h) and topo.may_write(h, d)):
+            return h
+    return None
+
+
+def _plane_relayed(j):
+    return PLANES[j][0] in RELAY
+
+
+def _helper_program(g, core, T, topo, sender, dst):
+    rid, pid = topo.addr(dst, core)
+    mask = topo.mask(core, dst)
+    n_hop = _engines(topo.mask(sender, core) & ~topo.mask(sender, dst))
+    calls = 0
+    for k in RELAY:
+        for j, (k0, k1) in enumerate(PLANES):
+            if k1 == k:
+                a, b = KT * GROUPS[k0][0], KT * GROUPS[k1][1]
+                g.wait_ge(T.sem["hp%d" % j], n_hop)
+                g.remote_dma(out_ap=T.rs[:, a:b], in_ap=T.rs[:, a:b], remote_sem=T.sem["ap%d" % j],
+                             local_sem=T.sem.sent, pid=pid, routing_id=rid, dma_engine_mask=mask)
+                calls += 1
+        a, b = KT * GROUPS[k][0], KT * GROUPS[k][1]
+        g.wait_ge(T.sem["hc%d" % k], n_hop)
+        g.remote_dma(out_ap=T.rq[:, a:b].bitcast(dt.uint8), in_ap=T.rq[:, a:b].bitcast(dt.uint8),
+                     remote_sem=T.sem["ac%d" % k], local_sem=T.sem.sent, pid=pid, routing_id=rid,
+                     dma_engine_mask=mask)
+        calls += 1
+    g.wait_ge(T.sem.sent, calls * _engines(mask))
+
+
 def rank_program(g, core, T, topo):
+    frm = T.tables["FROM"]
     rank = T.rank_of(core)
     if rank is None:
+        for r, c in enumerate(T.cores):
+            d = T.cores[frm.index(r)]
+            if _helper(T, topo, c, d) == core:
+                _helper_program(g, core, T, topo, c, d)
         return
-    frm = T.tables["FROM"]
     src = T.cores[frm[rank]]
     dst = T.cores[frm.index(rank)]
     rid, pid = topo.addr(dst, core)
     mask = topo.mask(core, dst)
-    n_out, n_in = _engines(mask), _engines(topo.mask(src, core))
+    hlp = _helper(T, topo, core, dst)
+    hrid, hpid = topo.addr(hlp, core)
+    hmask = topo.mask(core, hlp) & ~mask
+    n_dir = _engines(topo.mask(src, core))
+    n_rel = _engines(topo.mask(_helper(T, topo, src, core), core))
     loaders = (g.sync, g.scalar)
 
     for k, (c0, c1) in enumerate(GROUPS):
@@ -59,36 +105,52 @@ def rank_program(g, core, T, topo):
         g.vector.quantize_mx(T.wq[:, 128 * t:128 * t + 128], T.ws[:, 128 * t:128 * t + 128],
                              T.wb[:, 512 * t:512 * t + 512]).then_inc(T.sem.qw, 1)
 
+    left = 0
     for k, (c0, c1) in enumerate(GROUPS):
         g.wait_ge(T.sem["q%d" % k], KT)
         for j, (k0, k1) in enumerate(PLANES):
             if k1 == k:
                 a, b = KT * GROUPS[k0][0], KT * GROUPS[k1][1]
-                g.remote_dma(out_ap=T.rs[:, a:b], in_ap=T.xs[:, a:b], remote_sem=T.sem["ap%d" % j],
-                             local_sem=T.sem.sent, pid=pid, routing_id=rid, dma_engine_mask=mask)
+                if _plane_relayed(j):
+                    g.remote_dma(out_ap=T.rs[:, a:b], in_ap=T.xs[:, a:b], remote_sem=T.sem["hp%d" % j],
+                                 local_sem=T.sem.sent, pid=hpid, routing_id=hrid, dma_engine_mask=hmask)
+                    left += _engines(hmask)
+                else:
+                    g.remote_dma(out_ap=T.rs[:, a:b], in_ap=T.xs[:, a:b], remote_sem=T.sem["ap%d" % j],
+                                 local_sem=T.sem.sent, pid=pid, routing_id=rid, dma_engine_mask=mask)
+                    left += _engines(mask)
         a, b = KT * c0, KT * c1
-        g.remote_dma(out_ap=T.rq[:, a:b].bitcast(dt.uint8), in_ap=T.xq[:, a:b].bitcast(dt.uint8),
-                     remote_sem=T.sem["ac%d" % k], local_sem=T.sem.sent, pid=pid, routing_id=rid,
-                     dma_engine_mask=mask)
+        if k in RELAY:
+            g.remote_dma(out_ap=T.rq[:, a:b].bitcast(dt.uint8), in_ap=T.xq[:, a:b].bitcast(dt.uint8),
+                         remote_sem=T.sem["hc%d" % k], local_sem=T.sem.sent, pid=hpid, routing_id=hrid,
+                         dma_engine_mask=hmask)
+            left += _engines(hmask)
+        else:
+            g.remote_dma(out_ap=T.rq[:, a:b].bitcast(dt.uint8), in_ap=T.xq[:, a:b].bitcast(dt.uint8),
+                         remote_sem=T.sem["ac%d" % k], local_sem=T.sem.sent, pid=pid, routing_id=rid,
+                         dma_engine_mask=mask)
+            left += _engines(mask)
 
     g.tensor.wait_ge(T.sem.qw, KT)
-    for k, (c0, c1) in enumerate(GROUPS):
+    for k in MULT:
+        c0, c1 = GROUPS[k]
         n = c1 - c0
-        g.tensor.wait_ge(T.sem["ac%d" % k], n_in)
+        g.tensor.wait_ge(T.sem["ac%d" % k], n_rel if k in RELAY else n_dir)
         for j, (k0, k1) in enumerate(PLANES):
-            if k0 == k:
-                g.tensor.wait_ge(T.sem["ap%d" % j], n_in)
+            if k0 <= k <= k1:
+                g.tensor.wait_ge(T.sem["ap%d" % j], n_rel if _plane_relayed(j) else n_dir)
         for t in range(KT):
             p = KT * c0 + t * n
             g.tensor.matmul_mx(T.ps[:, 512 * k:512 * k + n], T.wq[:, 128 * t:128 * t + 128],
                                T.ws[:, 128 * t:128 * t + 128], T.rq[:, p:p + n], T.rs[:, p:p + n],
                                t == 0, t == KT - 1).then_inc(T.sem["mm%d" % k], 1)
 
-    for k, (c0, c1) in enumerate(GROUPS):
+    for k in MULT:
+        c0, c1 = GROUPS[k]
         n = c1 - c0
         g.vector.wait_ge(T.sem["mm%d" % k], KT)
         g.vector.tensor_copy(T.yb[:, c0:c1], T.ps[:, 512 * k:512 * k + n]).then_inc(T.sem["cp%d" % k], 1)
         g.sync.wait_ge(T.sem["cp%d" % k], 1)
         g.sync.dma_start(T.y[:, c0:c1], T.yb[:, c0:c1]).then_inc(T.sem.st, 16)
     g.sync.wait_ge(T.sem.st, 16 * G)
-    g.wait_ge(T.sem.sent, (G + len(PLANES)) * n_out)
+    g.wait_ge(T.sem.sent, left)

from concourse.mybir import dt

NC = 512
KT = 2
GROUPS = [(0, 128), (128, 256), (256, 384), (384, 512)]
RELAY = (1,)
PLANES = [(0, 0), (1, 1), (2, 3)]
MULT = [0, 2, 1, 3]
G = len(GROUPS)

SCRATCH = {
    "xb": ("sbuf", [128, KT * 4 * NC], "bfloat16"),
    "wb": ("sbuf", [128, KT * 512], "bfloat16"),
    "xq": ("sbuf", [128, KT * NC], "float8_e4m3fn_x4"),
    "xs": ("sbuf", [128, KT * NC], "uint8"),
    "wq": ("sbuf", [128, KT * 128], "float8_e4m3fn_x4"),
    "ws": ("sbuf", [128, KT * 128], "uint8"),
    "rq": ("sbuf", [128, KT * NC], "float8_e4m3fn_x4"),
    "rs": ("sbuf", [128, KT * NC], "uint8"),
    "ps": ("psum", [128, 512 * G], "float32"),
    "yb": ("sbuf", [128, NC], "float32"),
}
SEMAPHORES = (["lx%d_%d" % (k, t) for k in range(G) for t in range(KT)]
              + ["q%d" % k for k in range(G)] + ["ac%d" % k for k in range(G)]
              + ["ap%d" % j for j in range(len(PLANES))]
              + ["hc%d" % k for k in range(G)] + ["hp%d" % j for j in range(len(PLANES))]
              + ["mm%d" % k for k in range(G)] + ["cp%d" % k for k in range(G)]
              + ["lw", "qw", "st", "sent"])


def _engines(mask):
    return bin(mask).count("1")


def _helper(T, topo, c, d):
    hosts = 1 + max(topo.host(k) for k in T.cores)
    for h in range(hosts * topo.CORES_PER_HOST):
        if (topo.host(h) == topo.host(c) and topo.chip(h) == topo.chip(c) and h not in T.cores
                and topo.die(h) != topo.die(c) and topo.may_write(c, h) and topo.may_write(h, d)):
            return h
    return None


def _plane_relayed(j):
    return PLANES[j][0] in RELAY


def _helper_program(g, core, T, topo, sender, dst):
    rid, pid = topo.addr(dst, core)
    mask = topo.mask(core, dst)
    n_hop = _engines(topo.mask(sender, core) & ~topo.mask(sender, dst))
    calls = 0
    for k in RELAY:
        for j, (k0, k1) in enumerate(PLANES):
            if k1 == k:
                a, b = KT * GROUPS[k0][0], KT * GROUPS[k1][1]
                g.wait_ge(T.sem["hp%d" % j], n_hop)
                g.remote_dma(out_ap=T.rs[:, a:b], in_ap=T.rs[:, a:b], remote_sem=T.sem["ap%d" % j],
                             local_sem=T.sem.sent, pid=pid, routing_id=rid, dma_engine_mask=mask)
                calls += 1
        a, b = KT * GROUPS[k][0], KT * GROUPS[k][1]
        g.wait_ge(T.sem["hc%d" % k], n_hop)
        g.remote_dma(out_ap=T.rq[:, a:b].bitcast(dt.uint8), in_ap=T.rq[:, a:b].bitcast(dt.uint8),
                     remote_sem=T.sem["ac%d" % k], local_sem=T.sem.sent, pid=pid, routing_id=rid,
                     dma_engine_mask=mask)
        calls += 1
    g.wait_ge(T.sem.sent, calls * _engines(mask))


def rank_program(g, core, T, topo):
    frm = T.tables["FROM"]
    rank = T.rank_of(core)
    if rank is None:
        for r, c in enumerate(T.cores):
            d = T.cores[frm.index(r)]
            if _helper(T, topo, c, d) == core:
                _helper_program(g, core, T, topo, c, d)
        return
    src = T.cores[frm[rank]]
    dst = T.cores[frm.index(rank)]
    rid, pid = topo.addr(dst, core)
    mask = topo.mask(core, dst)
    hlp = _helper(T, topo, core, dst)
    hrid, hpid = topo.addr(hlp, core)
    hmask = topo.mask(core, hlp) & ~mask
    n_dir = _engines(topo.mask(src, core))
    n_rel = _engines(topo.mask(_helper(T, topo, src, core), core))
    loaders = (g.sync, g.scalar)

    for k, (c0, c1) in enumerate(GROUPS):
        for t in range(KT):
            a, b = 4 * NC * t + 4 * c0, 4 * NC * t + 4 * c1
            loaders[t % 2].dma_start(T.xb[:, a:b], T.x[:, a:b]).then_inc(T.sem["lx%d_%d" % (k, t)], 16)
    g.sync.dma_start(T.wb[:, :], T.w[:, :]).then_inc(T.sem.lw, 16)

    for k, (c0, c1) in enumerate(GROUPS):
        n = c1 - c0
        for t in range(KT):
            a, b = 4 * NC * t + 4 * c0, 4 * NC * t + 4 * c1
            p = KT * c0 + t * n
            g.vector.wait_ge(T.sem["lx%d_%d" % (k, t)], 16)
            g.vector.quantize_mx(T.xq[:, p:p + n], T.xs[:, p:p + n], T.xb[:, a:b]).then_inc(T.sem["q%d" % k], 1)
    g.vector.wait_ge(T.sem.lw, 16)
    for t in range(KT):
        g.vector.quantize_mx(T.wq[:, 128 * t:128 * t + 128], T.ws[:, 128 * t:128 * t + 128],
                             T.wb[:, 512 * t:512 * t + 512]).then_inc(T.sem.qw, 1)

    left = 0
    for k, (c0, c1) in enumerate(GROUPS):
        g.wait_ge(T.sem["q%d" % k], KT)
        for j, (k0, k1) in enumerate(PLANES):
            if k1 == k:
                a, b = KT * GROUPS[k0][0], KT * GROUPS[k1][1]
                if _plane_relayed(j):
                    g.remote_dma(out_ap=T.rs[:, a:b], in_ap=T.xs[:, a:b], remote_sem=T.sem["hp%d" % j],
                                 local_sem=T.sem.sent, pid=hpid, routing_id=hrid, dma_engine_mask=hmask)
                    left += _engines(hmask)
                else:
                    g.remote_dma(out_ap=T.rs[:, a:b], in_ap=T.xs[:, a:b], remote_sem=T.sem["ap%d" % j],
                                 local_sem=T.sem.sent, pid=pid, routing_id=rid, dma_engine_mask=mask)
                    left += _engines(mask)
        a, b = KT * c0, KT * c1
        if k in RELAY:
            g.remote_dma(out_ap=T.rq[:, a:b].bitcast(dt.uint8), in_ap=T.xq[:, a:b].bitcast(dt.uint8),
                         remote_sem=T.sem["hc%d" % k], local_sem=T.sem.sent, pid=hpid, routing_id=hrid,
                         dma_engine_mask=hmask)
            left += _engines(hmask)
        else:
            g.remote_dma(out_ap=T.rq[:, a:b].bitcast(dt.uint8), in_ap=T.xq[:, a:b].bitcast(dt.uint8),
                         remote_sem=T.sem["ac%d" % k], local_sem=T.sem.sent, pid=pid, routing_id=rid,
                         dma_engine_mask=mask)
            left += _engines(mask)

    g.tensor.wait_ge(T.sem.qw, KT)
    for k in MULT:
        c0, c1 = GROUPS[k]
        n = c1 - c0
        g.tensor.wait_ge(T.sem["ac%d" % k], n_rel if k in RELAY else n_dir)
        for j, (k0, k1) in enumerate(PLANES):
            if k0 <= k <= k1:
                g.tensor.wait_ge(T.sem["ap%d" % j], n_rel if _plane_relayed(j) else n_dir)
        for t in range(KT):
            p = KT * c0 + t * n
            g.tensor.matmul_mx(T.ps[:, 512 * k:512 * k + n], T.wq[:, 128 * t:128 * t + 128],
                               T.ws[:, 128 * t:128 * t + 128], T.rq[:, p:p + n], T.rs[:, p:p + n],
                               t == 0, t == KT - 1).then_inc(T.sem["mm%d" % k], 1)

    for k in MULT:
        c0, c1 = GROUPS[k]
        n = c1 - c0
        g.vector.wait_ge(T.sem["mm%d" % k], KT)
        g.vector.tensor_copy(T.yb[:, c0:c1], T.ps[:, 512 * k:512 * k + n]).then_inc(T.sem["cp%d" % k], 1)
        g.sync.wait_ge(T.sem["cp%d" % k], 1)
        g.sync.dma_start(T.y[:, c0:c1], T.yb[:, c0:c1]).then_inc(T.sem.st, 16)
    g.sync.wait_ge(T.sem.st, 16 * G)
    g.wait_ge(T.sem.sent, left)
